import numpy as np
import ml_dtypes


def mxq(x, axis, fmt="e4m3"):
    dtype, down = {"e4m3": (ml_dtypes.float8_e4m3fn, 7), "e5m2": (ml_dtypes.float8_e5m2, 14)}[fmt]
    v = np.moveaxis(np.asarray(x, np.float32).astype(ml_dtypes.bfloat16).astype(np.float64), axis, -1)
    blocks = v.reshape(v.shape[:-1] + (-1, 32))
    amax = np.abs(blocks).max(-1, keepdims=True)
    byte = np.maximum(np.where(amax > 0, np.frexp(amax)[1] - 1 + 127, 0) - down, 1)
    scale = np.exp2(byte - 127.0)
    codes = (blocks / scale).astype(np.float32).astype(dtype).astype(np.float64)
    return np.moveaxis((codes * scale).reshape(v.shape), -1, axis)


WIDE = False


def mx_kscale(k):
    if not WIDE:
        return np.ones(k)
    levels = np.array([30, -30])
    if k % 512:
        return np.exp2(np.random.permutation(np.resize(levels, k // 32))).repeat(32)
    a = np.empty((k // 512, 16))
    for p in range(k // 512):
        a[p, :8] = np.random.permutation(np.resize(levels, 8))
        for g in range(8):
            far = levels[np.abs(levels - a[p, g]) >= 10]
            a[p, g + 8] = far[np.random.randint(len(far))]
    return np.exp2(a.ravel()).repeat(32)


def f64(x):
    return np.asarray(x).astype(np.float64)


def striped(idx):
    return np.tile(np.asarray(idx).reshape(-1, 16).T, (8, 1)).astype(np.uint16)


def unstriped(offs):
    return offs[:16].T.reshape(-1).astype(np.int64)


def striped8(idx):
    return np.asarray(idx).reshape(8, -1, 16).transpose(0, 2, 1).reshape(128, -1).astype(np.uint16)


def unstriped8(offs):
    return offs.reshape(8, 16, -1).transpose(0, 2, 1).reshape(8, -1).astype(np.int64)


def pick8(x, idx, run):
    r = np.arange(len(x))
    return x[r[:, None], idx[r % (8 * run) // run]]


E2M1 = np.array([0.0, 0.5, 1.0, 1.5, 2.0, 3.0, 4.0, 6.0, -0.0, -0.5, -1.0, -1.5, -2.0, -3.0, -4.0, -6.0])


def pack_weight(w, fmt):
    k, n = w.shape
    w = f64(np.asarray(w, np.float32).astype(ml_dtypes.bfloat16)).reshape(k // 32, 32, n)
    amax = np.abs(w).max(1)
    if fmt in ("e4m3", "e5m2"):
        byte = np.frexp(amax)[1] - 1 + 127 - (7 if fmt == "e4m3" else 14)
    else:
        mant, ex = np.frexp(amax / 6.0)
        byte = np.where(mant > 0.5, ex, ex - 1) + 127
    byte = np.clip(np.where(amax > 0, byte, 1), 1, 254)
    scaled = (w * np.exp2(127.0 - byte)[:, None, :]).reshape(k, n).astype(np.float32)
    by_word = np.ascontiguousarray(scaled.reshape(k // 512, 128, 4, n).transpose(0, 1, 3, 2))
    if fmt in ("e4m3", "e5m2"):
        words = by_word.astype(ml_dtypes.float8_e4m3fn if fmt == "e4m3" else ml_dtypes.float8_e5m2).view(np.uint8)
    else:
        c = by_word.astype(ml_dtypes.float4_e2m1fn).view(np.uint8) & 0xF
        words = (c[..., 0::2] | (c[..., 1::2] << 4)).reshape(k // 512, 128, 2 * n)
    return np.ascontiguousarray(words), np.ascontiguousarray(byte.astype(np.uint8).reshape(k // 512, 16, n))


def unpack_weight(words, scales, fmt):
    g, _, n = scales.shape
    words = np.ascontiguousarray(words).reshape(g, 128, n, -1)
    if fmt in ("e4m3", "e5m2"):
        vals = words.view(ml_dtypes.float8_e4m3fn if fmt == "e4m3" else ml_dtypes.float8_e5m2).astype(np.float64)
    else:
        nib = np.empty((g, 128, n, 4), np.uint8)
        nib[..., 0::2] = words & 0xF
        nib[..., 1::2] = words >> 4
        vals = E2M1[nib]
    vals = vals * np.repeat(np.exp2(scales.astype(np.float64) - 127.0), 8, axis=1)[..., None]
    return vals.transpose(0, 1, 3, 2).reshape(g * 512, n)


def sigmoid(v):
    return 1.0 / (1.0 + np.exp(-v))


K, T, J, R, V, M, Q, O, D, N, U, E = 512, 1024, 256, 512, 1024, 512, 128, 128, 256, 256, 128, 512


def setup_inputs():
    n = np.random.standard_normal
    idx = np.random.permutation(V)[:R]
    idx2 = np.random.permutation(T)[:J]
    idx3 = np.stack([np.random.permutation(J)[:O] for _ in range(8)])
    idx4 = np.stack([np.random.permutation(J)[:O] for _ in range(8)])
    idx5 = np.random.permutation(D)[:U]
    idx6 = np.random.permutation(D)[:U]
    idx7 = np.random.permutation(E)[:U]
    fk = mx_kscale(K)
    fm = mx_kscale(M)
    fr = mx_kscale(R)
    xtp = pack_weight(n((K, T)) / fk[:, None], "e5m2")
    wtp = pack_weight(n((K, V)) * 1 / np.sqrt(K) * fk[:, None], "e2m1")
    xcp = pack_weight(n((M, Q)) / fm[:, None], "e5m2")
    wgp = pack_weight(n((M, R)) * 1 / np.sqrt(M) * fm[:, None] * fr, "e4m3")
    wbp = pack_weight(n((R, N)) * 1 / np.sqrt(R) / fr[:, None], "e2m1")
    return {
        "xt_words": xtp[0],
        "xt_scales": xtp[1],
        "wt_words": wtp[0],
        "wt_scales": wtp[1],
        "xc_words": xcp[0],
        "xc_scales": xcp[1],
        "wg_words": wgp[0],
        "wg_scales": wgp[1],
        "wb_words": wbp[0],
        "wb_scales": wbp[1],
        "so": (np.random.uniform(0.5, 1.6, (N, 1))).astype(np.float32),
        "sp": (np.random.uniform(0.6, 1.6, (N, 1))).astype(np.float32),
        "bo": (np.random.uniform(-1.0, 1.0, (N, 1))).astype(np.float32),
        "offs": striped(idx),
        "offs2": striped(idx2),
        "offs3": striped8(idx3),
        "offs4": striped8(idx4),
        "offs5": striped(idx5),
        "offs6": striped(idx6),
        "offs7": striped(idx7),
    }


def reference(xt_words, xt_scales, wt_words, wt_scales, xc_words, xc_scales, wg_words, wg_scales, wb_words, wb_scales, so, sp, bo, offs, offs2, offs3, offs4, offs5, offs6, offs7):
    idx = unstriped(offs)
    idx2 = unstriped(offs2)
    idx3 = unstriped8(offs3)
    idx4 = unstriped8(offs4)
    idx5 = unstriped(offs5)
    idx6 = unstriped(offs6)
    idx7 = unstriped(offs7)
    xtu = unpack_weight(xt_words, xt_scales, "e5m2")
    wtu = unpack_weight(wt_words, wt_scales, "e2m1")
    xcu = unpack_weight(xc_words, xc_scales, "e5m2")
    wgu = unpack_weight(wg_words, wg_scales, "e4m3")
    wbu = unpack_weight(wb_words, wb_scales, "e2m1")
    wtidxg = wtu[:, idx]
    xtidx2g = xtu[:, idx2]
    a = wtidxg.T @ xtidx2g
    g0 = wgu.T @ xcu
    ga = g0[:, 0:1]
    gb = g0[:, 64:65]
    h1 = np.maximum(pick8(a, idx3, 64) * ga, pick8(a, idx4, 64) * gb)
    hid = np.concatenate([h1, g0], axis=1)
    hidq = mxq(hid, 0, "e4m3")
    p = wbu.T @ hidq
    m0 = p[:, idx5] * f64(so) * sigmoid(p[:, idx6] * f64(sp) + f64(bo))
    y = np.zeros((N, E))
    y[:, idx7] = m0
    return y

@@ -1,0 +1,192 @@
+from contextlib import ExitStack
+
+import concourse.mybir as mybir
+from concourse.masks import make_identity
+
+F32 = mybir.dt.float32
+BF16 = mybir.dt.bfloat16
+I32 = mybir.dt.int32
+U32 = mybir.dt.uint32
+U16 = mybir.dt.uint16
+U8 = mybir.dt.uint8
+E4M3 = mybir.dt.float8_e4m3fn_x4
+E5M2 = mybir.dt.float8_e5m2_x4
+E2M1 = mybir.dt.float4_e2m1fn_x4
+ACT = mybir.ActivationFunctionType
+ALU = mybir.AluOpType
+
+P = 128
+T, J, R, V, Q, O, D, N, U, E = 1024, 256, 512, 1024, 128, 128, 256, 256, 128, 512
+FLOPS = 2 * 512 * (R * J + R * Q + N * D)
+
+
+def tile_list_ctxgroups_chosen_one_gatedposted_kernel(
+    tc, xt_words, xt_scales, wt_words, wt_scales, xc_words, xc_scales, wg_words, wg_scales,
+    wb_words, wb_scales, so, sp, bo, offs, offs2, offs3, offs4, offs5, offs6, offs7, out,
+):
+    nc = tc.nc
+    with ExitStack() as ctx:
+        lists = ctx.enter_context(tc.tile_pool(name="lists", bufs=1))
+        sb = ctx.enter_context(tc.tile_pool(name="sb", bufs=1))
+        ps = ctx.enter_context(tc.psum_pool(name="ps", bufs=1))
+
+        def load_list(src, name):
+            tile = lists.tile(list(src.shape), U16, name=name)
+            nc.sync.dma_start(tile[:], src)
+            return tile
+
+        def load_scale_rows(queue, plane, src):
+            for quad in range(4):
+                queue.dma_start(
+                    plane[32 * quad : 32 * quad + 4, :].bitcast(I32),
+                    src[0, 4 * quad : 4 * quad + 4, :].bitcast(I32),
+                )
+
+        wt_s = sb.tile([P, V], U8, name="wt_s", align_bytes=64)
+        xt_s = sb.tile([P, T], U8, name="xt_s", align_bytes=64)
+        g_s = sb.tile([P, Q + R], U8, name="ctx_s", align_bytes=64)
+        wb_s = sb.tile([P, N], U8, name="wb_s", align_bytes=64)
+        xc_s = g_s[:, 0:Q]
+        wg_s = g_s[:, Q : Q + R]
+        stage = sb.tile([4, 4, Q + R], U8, name="stage", align_bytes=64)
+
+        wt_w = sb.tile([P, V], U16, name="wt_w", align_bytes=64)
+        xt_w = sb.tile([P, T], U32, name="xt_w", align_bytes=64)
+        wg_w = sb.tile([P, R], U32, name="wg_w", align_bytes=64)
+        xc_w = sb.tile([P, Q], U32, name="xc_w", align_bytes=64)
+        wb_w = sb.tile([P, N], U16, name="wb_w", align_bytes=64)
+
+        def load_rows(plane, src, quad):
+            nc.sync.dma_start(
+                plane[32 * quad : 32 * quad + 4, :].bitcast(I32),
+                src[0, 4 * quad : 4 * quad + 4, :].bitcast(I32),
+            )
+
+        nc.scalar.dma_start(wt_w[:].bitcast(I32), wt_words[0].bitcast(I32))
+        nc.gpsimd.memset(wt_s[:].bitcast(I32), 0)
+        nc.gpsimd.memset(xt_s[:].bitcast(I32), 0)
+        nc.vector.memset(g_s[:].bitcast(I32), 0)
+        nc.vector.memset(wb_s[:].bitcast(I32), 0)
+
+        nc.sync.dma_start(stage[:, :, 0:Q].bitcast(I32), xc_scales[0].rearrange("(q r) n -> r q n", r=4).bitcast(I32))
+        nc.sync.dma_start(stage[:, :, Q : Q + R].bitcast(I32), wg_scales[0].rearrange("(q r) n -> r q n", r=4).bitcast(I32))
+        l1 = load_list(offs, "l1")
+        l2 = load_list(offs2, "l2")
+        load_rows(wt_s, wt_scales, 0)
+        load_rows(wt_s, wt_scales, 1)
+        nc.sync.dma_start(xt_w[:].bitcast(I32), xt_words[0].rearrange("p n t -> p (n t)").bitcast(I32))
+        load_rows(wt_s, wt_scales, 2)
+        load_rows(wt_s, wt_scales, 3)
+        nc.sync.dma_start(xc_w[:].bitcast(I32), xc_words[0].rearrange("p n t -> p (n t)").bitcast(I32))
+        nc.sync.dma_start(wg_w[:].bitcast(I32), wg_words[0].rearrange("p n t -> p (n t)").bitcast(I32))
+        load_scale_rows(nc.sync, xt_s, xt_scales)
+        l3 = load_list(offs3, "l3")
+        l4 = load_list(offs4, "l4")
+        nc.sync.dma_start(wb_w[:].bitcast(I32), wb_words[0].bitcast(I32))
+        load_scale_rows(nc.sync, wb_s, wb_scales)
+        cols = {}
+        for name, src in (("so", so), ("sp", sp), ("bo", bo)):
+            cols[name] = sb.tile([P, 2], F32, name=name + "_c")
+            with nc.allow_non_contiguous_dma(reason="one value a partition"):
+                nc.sync.dma_start(cols[name][:], src.rearrange("(c p) o -> p (c o)", p=P))
+        l5 = load_list(offs5, "l5")
+        l6 = load_list(offs6, "l6")
+        l7 = load_list(offs7, "l7")
+
+        ident = sb.tile([P, P], F32, name="ident")
+        make_identity(nc, ident[:])
+
+        pages = [sb.tile([P, E], F32, name="page%d" % c) for c in range(2)]
+        for c in range(2):
+            nc.vector.memset(pages[c][:], 0.0)
+
+        wt_wg = sb.tile([P, R], U16, name="wt_wg", align_bytes=64)
+        xt_wg = [sb.tile([P, P], U32, name="xt_wg%d" % h, align_bytes=64) for h in range(2)]
+        xt_sg = [sb.tile([P, P], U8, name="xt_sg%d" % h, align_bytes=64) for h in range(2)]
+        wt_sd = sb.tile([P, R], U8, name="wt_sd", align_bytes=64)
+        wt_wd = sb.tile([P, R], U16, name="wt_wd", align_bytes=64)
+        for quad in range(4):
+            nc.vector.tensor_copy(g_s[32 * quad : 32 * quad + 4, :].bitcast(I32), stage[:, quad, :].bitcast(I32))
+        nc.vector.tensor_copy(wt_wg[:], wt_w[:].indirect(l1[:]))
+        nc.vector.tensor_copy(xt_wg[0][:], xt_w[:].indirect(l2[:, 0:8]))
+        nc.vector.tensor_copy(
+            wt_wd[:].rearrange("p (t c i) -> p c t i", t=4, i=8),
+            wt_wg[:].rearrange("p (c i t) -> p c t i", t=4, i=8),
+        )
+        nc.vector.tensor_copy(wt_sd[:].rearrange("p (t m) -> p m t", t=4), wt_s[:].indirect(l1[:]))
+        nc.vector.tensor_copy(xt_wg[1][:], xt_w[:].indirect(l2[:, 8:16]))
+        nc.vector.tensor_copy(xt_sg[0][:], xt_s[:].indirect(l2[:, 0:8]))
+        nc.vector.tensor_copy(xt_sg[1][:], xt_s[:].indirect(l2[:, 8:16]))
+
+        gT_ps = ps.tile([P, R], F32, name="gT_ps", tag="b0")
+        nc.tensor.matmul_mx(gT_ps[:], lhsT=xc_w[:].bitcast(E5M2), lhsT_scale=xc_s, rhs=wg_w[:].bitcast(E4M3),
+                            rhs_scale=wg_s, start=True, stop=True)
+        gT = sb.tile([P, 4, P], F32, name="gT")
+        nc.scalar.activation(gT[:], gT_ps[:].rearrange("q (m t) -> q t m", t=4), ACT.Copy)
+        g_ps = ps.tile([P, 4, Q], F32, name="g_ps", tag="b1")
+        for t in range(4):
+            nc.tensor.transpose(g_ps[:, t, :], gT[:, t, :], ident[:])
+        gains = sb.tile([P, 4, 2], F32, name="gains")
+        nc.scalar.copy(gains[:], g_ps[:, :, 0:Q:64])
+        g_bf = sb.tile([P, Q, 4], BF16, name="g_bf", align_bytes=64)
+
+        a_sb = [sb.tile([P, J], F32, name="a_sb%d" % t) for t in range(4)]
+
+        def slot_product(dst, t, h):
+            nc.tensor.matmul_mx(dst, lhsT=wt_wd[:, P * t : P * (t + 1)].bitcast(E2M1),
+                                lhsT_scale=wt_sd[:, P * t : P * (t + 1)], rhs=xt_wg[h][:].bitcast(E5M2),
+                                rhs_scale=xt_sg[h][:], start=True, stop=True)
+
+        for t in range(2):
+            a_ps = ps.tile([P, P], F32, name="a_ps0%d" % t, tag="b%d" % (2 + t))
+            slot_product(a_ps[:], t, 0)
+            nc.scalar.copy(a_sb[t][:, 0:P], a_ps[:])
+        for t in range(2):
+            a_ps = ps.tile([P, P], F32, name="a_ps1%d" % t, tag="b%d" % (4 + t))
+            slot_product(a_ps[:], t, 1)
+            nc.vector.tensor_copy(a_sb[t][:, P:J], a_ps[:])
+        for t in range(2, 4):
+            a_ps = ps.tile([P, J], F32, name="a_ps%d" % t, tag="b%d" % (4 + t))
+            for h in range(2):
+                slot_product(a_ps[:, P * h : P * (h + 1)], t, h)
+            nc.vector.tensor_copy(a_sb[t][:], a_ps[:])
+
+        nc.vector.tensor_copy(g_bf[:], g_ps[:].rearrange("p t q -> p q t"))
+        p_sb = [sb.tile([P, D], F32, name="p_sb%d" % c) for c in range(2)]
+
+        def output_product(x_bf, name, tags, d0):
+            codes = sb.tile([P, P], U32, name=name + "_w", align_bytes=64)
+            plane = sb.tile([P, P], U8, name=name + "_s", align_bytes=64)
+            nc.vector.quantize_mx(codes[:].bitcast(E4M3), plane[:], x_bf[:].rearrange("p d t -> p (d t)"))
+            for c in range(2):
+                p_ps = ps.tile([P, P], F32, name="%s_ps%d" % (name, c), tag=tags[c])
+                nc.tensor.matmul_mx(p_ps[:], lhsT=wb_w[:, P * c : P * (c + 1)].bitcast(E2M1),
+                                    lhsT_scale=wb_s[:, P * c : P * (c + 1)], rhs=codes[:].bitcast(E4M3),
+                                    rhs_scale=plane[:], start=True, stop=True)
+                nc.vector.tensor_copy(p_sb[c][:, d0 : d0 + P], p_ps[:])
+
+        h_bf = sb.tile([P, O, 4], BF16, name="h_bf", align_bytes=64)
+        for u in range(2):
+            first = sb.tile([P, 2, O], F32, name="first%d" % u)
+            second = sb.tile([P, 2, O], F32, name="second%d" % u)
+            for s in range(2):
+                t = 2 * u + s
+                nc.scalar.activation(first[:, s, :], a_sb[t][:].indirect(l3[:]), ACT.Copy, scale=gains[:, t, 0:1])
+                nc.scalar.activation(second[:, s, :], a_sb[t][:].indirect(l4[:]), ACT.Copy, scale=gains[:, t, 1:2])
+            nc.vector.tensor_tensor(h_bf[:, :, 2 * u : 2 * u + 2], first[:].rearrange("p s o -> p o s"),
+                                    second[:].rearrange("p s o -> p o s"), ALU.max)
+            if u == 0:
+                output_product(g_bf, "g", ("b2", "b3"), O)
+        output_product(h_bf, "h", ("b0", "b1"), 0)
+
+        H = U // 2
+        for c in range(2):
+            for half in range(2):
+                gate = sb.tile([P, H], F32, name="gate%d%d" % (c, half))
+                val = sb.tile([P, H], F32, name="val%d%d" % (c, half))
+                cut = slice(4 * half, 4 * half + 4)
+                nc.scalar.activation(gate[:], p_sb[c][:].indirect(l6[:, cut]), ACT.Sigmoid,
+                                     bias=cols["bo"][:, c : c + 1], scale=cols["sp"][:, c : c + 1])
+                nc.scalar.activation(val[:], p_sb[c][:].indirect(l5[:, cut]), ACT.Copy, scale=cols["so"][:, c : c + 1])
+                nc.vector.tensor_tensor(pages[c][:].indirect(l7[:, cut]), val[:], gate[:], ALU.mult)
+            nc.sync.dma_start(out[P * c : P * (c + 1), :], pages[c][:])

@@ -65,6 +65,9 @@ def tile_list_ctxgroups_chosen_one_gatedposted_kernel(
         nc.scalar.dma_start(wt_w[:].bitcast(I32), wt_words[0].bitcast(I32))
         nc.gpsimd.memset(wt_s[:].bitcast(I32), 0)
         nc.gpsimd.memset(xt_s[:].bitcast(I32), 0)
+        warm = sb.tile([P, 2], F32, name="warm")
+        nc.vector.memset(warm[:, 0:1], 0.0)
+        nc.scalar.activation(warm[:, 1:2], warm[:, 0:1], ACT.Sigmoid)
         nc.vector.memset(g_s[:].bitcast(I32), 0)
         nc.vector.memset(wb_s[:].bitcast(I32), 0)
 

@@ -56,32 +56,23 @@ def tile_list_ctxgroups_chosen_one_gatedposted_kernel(
         xc_w = sb.tile([P, Q], U32, name="xc_w", align_bytes=64)
         wb_w = sb.tile([P, N], U16, name="wb_w", align_bytes=64)
 
-        def load_rows(plane, src, quad):
-            nc.sync.dma_start(
-                plane[32 * quad : 32 * quad + 4, :].bitcast(I32),
-                src[0, 4 * quad : 4 * quad + 4, :].bitcast(I32),
-            )
-
         nc.scalar.dma_start(wt_w[:].bitcast(I32), wt_words[0].bitcast(I32))
-        nc.gpsimd.memset(wt_s[:].bitcast(I32), 0)
-        nc.gpsimd.memset(xt_s[:].bitcast(I32), 0)
         warm = sb.tile([P, 2], F32, name="warm")
         nc.vector.memset(warm[:, 0:1], 0.0)
         nc.scalar.activation(warm[:, 1:2], warm[:, 0:1], ACT.Sigmoid)
         nc.vector.memset(g_s[:].bitcast(I32), 0)
+        nc.vector.memset(wt_s[:].bitcast(I32), 0)
+        nc.vector.memset(xt_s[:].bitcast(I32), 0)
         nc.vector.memset(wb_s[:].bitcast(I32), 0)
 
         nc.sync.dma_start(stage[:, :, 0:Q].bitcast(I32), xc_scales[0].rearrange("(q r) n -> r q n", r=4).bitcast(I32))
         nc.sync.dma_start(stage[:, :, Q : Q + R].bitcast(I32), wg_scales[0].rearrange("(q r) n -> r q n", r=4).bitcast(I32))
         l1 = load_list(offs, "l1")
-        l2 = load_list(offs2, "l2")
-        load_rows(wt_s, wt_scales, 0)
-        load_rows(wt_s, wt_scales, 1)
-        nc.sync.dma_start(xt_w[:].bitcast(I32), xt_words[0].rearrange("p n t -> p (n t)").bitcast(I32))
-        load_rows(wt_s, wt_scales, 2)
-        load_rows(wt_s, wt_scales, 3)
         nc.sync.dma_start(xc_w[:].bitcast(I32), xc_words[0].rearrange("p n t -> p (n t)").bitcast(I32))
         nc.sync.dma_start(wg_w[:].bitcast(I32), wg_words[0].rearrange("p n t -> p (n t)").bitcast(I32))
+        l2 = load_list(offs2, "l2")
+        nc.sync.dma_start(xt_w[:].bitcast(I32), xt_words[0].rearrange("p n t -> p (n t)").bitcast(I32))
+        load_scale_rows(nc.sync, wt_s, wt_scales)
         load_scale_rows(nc.sync, xt_s, xt_scales)
         l3 = load_list(offs3, "l3")
         l4 = load_list(offs4, "l4")
@@ -107,19 +98,19 @@ def tile_list_ctxgroups_chosen_one_gatedposted_kernel(
         xt_wg = [sb.tile([P, P], U32, name="xt_wg%d" % h, align_bytes=64) for h in range(2)]
         xt_sg = [sb.tile([P, P], U8, name="xt_sg%d" % h, align_bytes=64) for h in range(2)]
         wt_sd = sb.tile([P, R], U8, name="wt_sd", align_bytes=64)
-        wt_wd = sb.tile([P, R], U16, name="wt_wd", align_bytes=64)
+        wt_wd = sb.tile([P, R], U16, name="wt_wd", tag="dealt", align_bytes=64)
         for quad in range(4):
             nc.vector.tensor_copy(g_s[32 * quad : 32 * quad + 4, :].bitcast(I32), stage[:, quad, :].bitcast(I32))
         nc.vector.tensor_copy(wt_wg[:], wt_w[:].indirect(l1[:]))
-        nc.vector.tensor_copy(xt_wg[0][:], xt_w[:].indirect(l2[:, 0:8]))
         nc.vector.tensor_copy(
             wt_wd[:].rearrange("p (t c i) -> p c t i", t=4, i=8),
             wt_wg[:].rearrange("p (c i t) -> p c t i", t=4, i=8),
         )
+        for h in range(2):
+            nc.vector.tensor_copy(xt_wg[h][:], xt_w[:].indirect(l2[:, 8 * h : 8 * h + 8]))
         nc.vector.tensor_copy(wt_sd[:].rearrange("p (t m) -> p m t", t=4), wt_s[:].indirect(l1[:]))
-        nc.vector.tensor_copy(xt_wg[1][:], xt_w[:].indirect(l2[:, 8:16]))
-        nc.vector.tensor_copy(xt_sg[0][:], xt_s[:].indirect(l2[:, 0:8]))
-        nc.vector.tensor_copy(xt_sg[1][:], xt_s[:].indirect(l2[:, 8:16]))
+        for h in range(2):
+            nc.vector.tensor_copy(xt_sg[h][:], xt_s[:].indirect(l2[:, 8 * h : 8 * h + 8]))
 
         gT_ps = ps.tile([P, R], F32, name="gT_ps", tag="b0")
         nc.tensor.matmul_mx(gT_ps[:], lhsT=xc_w[:].bitcast(E5M2), lhsT_scale=xc_s, rhs=wg_w[:].bitcast(E4M3),
@@ -129,9 +120,8 @@ def tile_list_ctxgroups_chosen_one_gatedposted_kernel(
         g_ps = ps.tile([P, 4, Q], F32, name="g_ps", tag="b1")
         for t in range(4):
             nc.tensor.transpose(g_ps[:, t, :], gT[:, t, :], ident[:])
-        gains = sb.tile([P, 4, 2], F32, name="gains")
-        nc.scalar.copy(gains[:], g_ps[:, :, 0:Q:64])
-        g_bf = sb.tile([P, Q, 4], BF16, name="g_bf", align_bytes=64)
+        g_sb = sb.tile([P, 4, Q], F32, name="g_sb")
+        nc.scalar.copy(g_sb[:], g_ps[:])
 
         a_sb = [sb.tile([P, J], F32, name="a_sb%d" % t) for t in range(4)]
 
@@ -140,21 +130,18 @@ def tile_list_ctxgroups_chosen_one_gatedposted_kernel(
                                 lhsT_scale=wt_sd[:, P * t : P * (t + 1)], rhs=xt_wg[h][:].bitcast(E5M2),
                                 rhs_scale=xt_sg[h][:], start=True, stop=True)
 
-        for t in range(2):
-            a_ps = ps.tile([P, P], F32, name="a_ps0%d" % t, tag="b%d" % (2 + t))
-            slot_product(a_ps[:], t, 0)
-            nc.scalar.copy(a_sb[t][:, 0:P], a_ps[:])
-        for t in range(2):
-            a_ps = ps.tile([P, P], F32, name="a_ps1%d" % t, tag="b%d" % (4 + t))
-            slot_product(a_ps[:], t, 1)
-            nc.vector.tensor_copy(a_sb[t][:, P:J], a_ps[:])
-        for t in range(2, 4):
-            a_ps = ps.tile([P, J], F32, name="a_ps%d" % t, tag="b%d" % (4 + t))
+        for h, engine_copy in enumerate((nc.scalar.copy, nc.vector.tensor_copy)):
+            a_ps = ps.tile([P, P], F32, name="a_ps0%d" % h, tag="b%d" % h)
+            slot_product(a_ps[:], 0, h)
+            engine_copy(a_sb[0][:, P * h : P * (h + 1)], a_ps[:])
+        for t in range(1, 4):
+            a_ps = ps.tile([P, J], F32, name="a_ps%d" % t, tag="b%d" % ((t + 1) % 2))
             for h in range(2):
                 slot_product(a_ps[:, P * h : P * (h + 1)], t, h)
             nc.vector.tensor_copy(a_sb[t][:], a_ps[:])
 
-        nc.vector.tensor_copy(g_bf[:], g_ps[:].rearrange("p t q -> p q t"))
+        g_bf = sb.tile([P, Q, 4], BF16, name="g_bf", tag="dealt", align_bytes=64)
+        nc.vector.tensor_copy(g_bf[:].rearrange("p (c i) t -> p c t i", i=4), g_sb[:].rearrange("p t (c i) -> p c t i", i=4))
         p_sb = [sb.tile([P, D], F32, name="p_sb%d" % c) for c in range(2)]
 
         def output_product(x_bf, name, tags, d0):
@@ -174,13 +161,13 @@ def tile_list_ctxgroups_chosen_one_gatedposted_kernel(
             second = sb.tile([P, 2, O], F32, name="second%d" % u)
             for s in range(2):
                 t = 2 * u + s
-                nc.scalar.activation(first[:, s, :], a_sb[t][:].indirect(l3[:]), ACT.Copy, scale=gains[:, t, 0:1])
-                nc.scalar.activation(second[:, s, :], a_sb[t][:].indirect(l4[:]), ACT.Copy, scale=gains[:, t, 1:2])
+                nc.scalar.activation(first[:, s, :], a_sb[t][:].indirect(l3[:]), ACT.Copy, scale=g_sb[:, t, 0:1])
+                nc.scalar.activation(second[:, s, :], a_sb[t][:].indirect(l4[:]), ACT.Copy, scale=g_sb[:, t, 64:65])
             nc.vector.tensor_tensor(h_bf[:, :, 2 * u : 2 * u + 2], first[:].rearrange("p s o -> p o s"),
                                     second[:].rearrange("p s o -> p o s"), ALU.max)
             if u == 0:
                 output_product(g_bf, "g", ("b2", "b3"), O)
-        output_product(h_bf, "h", ("b0", "b1"), 0)
+        output_product(h_bf, "h", ("b4", "b5"), 0)
 
         H = U // 2
         for c in range(2):

@@ -56,7 +56,9 @@ def tile_list_ctxgroups_chosen_one_gatedposted_kernel(
         xc_w = sb.tile([P, Q], U32, name="xc_w", align_bytes=64)
         wb_w = sb.tile([P, N], U16, name="wb_w", align_bytes=64)
 
-        nc.scalar.dma_start(wt_w[:].bitcast(I32), wt_words[0].bitcast(I32))
+        nc.scalar.dma_start(stage[:, :, Q : Q + R].bitcast(I32), wg_scales[0].rearrange("(q r) n -> r q n", r=4).bitcast(I32))
+        nc.sync.dma_start(stage[:, :, 0:Q].bitcast(I32), xc_scales[0].rearrange("(q r) n -> r q n", r=4).bitcast(I32))
+        nc.sync.dma_start(wt_w[:].bitcast(I32), wt_words[0].bitcast(I32))
         warm = sb.tile([P, 2], F32, name="warm")
         nc.vector.memset(warm[:, 0:1], 0.0)
         nc.scalar.activation(warm[:, 1:2], warm[:, 0:1], ACT.Sigmoid)
@@ -65,8 +67,6 @@ def tile_list_ctxgroups_chosen_one_gatedposted_kernel(
         nc.vector.memset(xt_s[:].bitcast(I32), 0)
         nc.vector.memset(wb_s[:].bitcast(I32), 0)
 
-        nc.sync.dma_start(stage[:, :, 0:Q].bitcast(I32), xc_scales[0].rearrange("(q r) n -> r q n", r=4).bitcast(I32))
-        nc.sync.dma_start(stage[:, :, Q : Q + R].bitcast(I32), wg_scales[0].rearrange("(q r) n -> r q n", r=4).bitcast(I32))
         l1 = load_list(offs, "l1")
         nc.sync.dma_start(xc_w[:].bitcast(I32), xc_words[0].rearrange("p n t -> p (n t)").bitcast(I32))
         nc.sync.dma_start(wg_w[:].bitcast(I32), wg_words[0].rearrange("p n t -> p (n t)").bitcast(I32))
@@ -169,14 +169,11 @@ def tile_list_ctxgroups_chosen_one_gatedposted_kernel(
                 output_product(g_bf, "g", ("b2", "b3"), O)
         output_product(h_bf, "h", ("b4", "b5"), 0)
 
-        H = U // 2
         for c in range(2):
-            for half in range(2):
-                gate = sb.tile([P, H], F32, name="gate%d%d" % (c, half))
-                val = sb.tile([P, H], F32, name="val%d%d" % (c, half))
-                cut = slice(4 * half, 4 * half + 4)
-                nc.scalar.activation(gate[:], p_sb[c][:].indirect(l6[:, cut]), ACT.Sigmoid,
-                                     bias=cols["bo"][:, c : c + 1], scale=cols["sp"][:, c : c + 1])
-                nc.scalar.activation(val[:], p_sb[c][:].indirect(l5[:, cut]), ACT.Copy, scale=cols["so"][:, c : c + 1])
-                nc.vector.tensor_tensor(pages[c][:].indirect(l7[:, cut]), val[:], gate[:], ALU.mult)
+            gate = sb.tile([P, U], F32, name="gate%d" % c)
+            val = sb.tile([P, U], F32, name="val%d" % c)
+            nc.scalar.activation(gate[:], p_sb[c][:].indirect(l6[:]), ACT.Sigmoid,
+                                 bias=cols["bo"][:, c : c + 1], scale=cols["sp"][:, c : c + 1])
+            nc.scalar.activation(val[:], p_sb[c][:].indirect(l5[:]), ACT.Copy, scale=cols["so"][:, c : c + 1])
+            nc.vector.tensor_tensor(pages[c][:].indirect(l7[:]), val[:], gate[:], ALU.mult)
             nc.sync.dma_start(out[P * c : P * (c + 1), :], pages[c][:])

from contextlib import ExitStack

import concourse.mybir as mybir
from concourse.masks import make_identity

F32 = mybir.dt.float32
BF16 = mybir.dt.bfloat16
I32 = mybir.dt.int32
U32 = mybir.dt.uint32
U16 = mybir.dt.uint16
U8 = mybir.dt.uint8
E4M3 = mybir.dt.float8_e4m3fn_x4
E5M2 = mybir.dt.float8_e5m2_x4
E2M1 = mybir.dt.float4_e2m1fn_x4
ACT = mybir.ActivationFunctionType
ALU = mybir.AluOpType

P = 128
T, J, R, V, Q, O, D, N, U, E = 1024, 256, 512, 1024, 128, 128, 256, 256, 128, 512
FLOPS = 2 * 512 * (R * J + R * Q + N * D)


def tile_list_ctxgroups_chosen_one_gatedposted_kernel(
    tc, xt_words, xt_scales, wt_words, wt_scales, xc_words, xc_scales, wg_words, wg_scales,
    wb_words, wb_scales, so, sp, bo, offs, offs2, offs3, offs4, offs5, offs6, offs7, out,
):
    nc = tc.nc
    with ExitStack() as ctx:
        lists = ctx.enter_context(tc.tile_pool(name="lists", bufs=1))
        sb = ctx.enter_context(tc.tile_pool(name="sb", bufs=1))
        ps = ctx.enter_context(tc.psum_pool(name="ps", bufs=1))

        def load_list(src, name):
            tile = lists.tile(list(src.shape), U16, name=name)
            nc.sync.dma_start(tile[:], src)
            return tile

        def load_scale_rows(queue, plane, src):
            for quad in range(4):
                queue.dma_start(
                    plane[32 * quad : 32 * quad + 4, :].bitcast(I32),
                    src[0, 4 * quad : 4 * quad + 4, :].bitcast(I32),
                )

        wt_s = sb.tile([P, V], U8, name="wt_s", align_bytes=64)
        xt_s = sb.tile([P, T], U8, name="xt_s", align_bytes=64)
        g_s = sb.tile([P, Q + R], U8, name="ctx_s", align_bytes=64)
        wb_s = sb.tile([P, N], U8, name="wb_s", align_bytes=64)
        xc_s = g_s[:, 0:Q]
        wg_s = g_s[:, Q : Q + R]
        stage = sb.tile([4, 4, Q + R], U8, name="stage", align_bytes=64)

        wt_w = sb.tile([P, V], U16, name="wt_w", align_bytes=64)
        xt_w = sb.tile([P, T], U32, name="xt_w", align_bytes=64)
        wg_w = sb.tile([P, R], U32, name="wg_w", align_bytes=64)
        xc_w = sb.tile([P, Q], U32, name="xc_w", align_bytes=64)
        wb_w = sb.tile([P, N], U16, name="wb_w", align_bytes=64)

        nc.scalar.dma_start(stage[:, :, Q : Q + R].bitcast(I32), wg_scales[0].rearrange("(q r) n -> r q n", r=4).bitcast(I32))
        nc.sync.dma_start(stage[:, :, 0:Q].bitcast(I32), xc_scales[0].rearrange("(q r) n -> r q n", r=4).bitcast(I32))
        nc.sync.dma_start(wt_w[:].bitcast(I32), wt_words[0].bitcast(I32))
        warm = sb.tile([P, 2], F32, name="warm")
        nc.vector.memset(warm[:, 0:1], 0.0)
        nc.scalar.activation(warm[:, 1:2], warm[:, 0:1], ACT.Sigmoid)
        nc.vector.memset(g_s[:].bitcast(I32), 0)
        nc.vector.memset(wt_s[:].bitcast(I32), 0)
        nc.vector.memset(xt_s[:].bitcast(I32), 0)
        nc.vector.memset(wb_s[:].bitcast(I32), 0)

        l1 = load_list(offs, "l1")
        nc.sync.dma_start(xc_w[:].bitcast(I32), xc_words[0].rearrange("p n t -> p (n t)").bitcast(I32))
        nc.sync.dma_start(wg_w[:].bitcast(I32), wg_words[0].rearrange("p n t -> p (n t)").bitcast(I32))
        l2 = load_list(offs2, "l2")
        nc.sync.dma_start(xt_w[:].bitcast(I32), xt_words[0].rearrange("p n t -> p (n t)").bitcast(I32))
        load_scale_rows(nc.sync, wt_s, wt_scales)
        load_scale_rows(nc.sync, xt_s, xt_scales)
        l3 = load_list(offs3, "l3")
        l4 = load_list(offs4, "l4")
        nc.sync.dma_start(wb_w[:].bitcast(I32), wb_words[0].bitcast(I32))
        load_scale_rows(nc.sync, wb_s, wb_scales)
        cols = {}
        for name, src in (("so", so), ("sp", sp), ("bo", bo)):
            cols[name] = sb.tile([P, 2], F32, name=name + "_c")
            with nc.allow_non_contiguous_dma(reason="one value a partition"):
                nc.sync.dma_start(cols[name][:], src.rearrange("(c p) o -> p (c o)", p=P))
        l5 = load_list(offs5, "l5")
        l6 = load_list(offs6, "l6")
        l7 = load_list(offs7, "l7")

        ident = sb.tile([P, P], F32, name="ident")
        make_identity(nc, ident[:])

        pages = [sb.tile([P, E], F32, name="page%d" % c) for c in range(2)]
        for c in range(2):
            nc.vector.memset(pages[c][:], 0.0)

        wt_wg = sb.tile([P, R], U16, name="wt_wg", align_bytes=64)
        xt_wg = [sb.tile([P, P], U32, name="xt_wg%d" % h, align_bytes=64) for h in range(2)]
        xt_sg = [sb.tile([P, P], U8, name="xt_sg%d" % h, align_bytes=64) for h in range(2)]
        wt_sd = sb.tile([P, R], U8, name="wt_sd", align_bytes=64)
        wt_wd = sb.tile([P, R], U16, name="wt_wd", tag="dealt", align_bytes=64)
        for quad in range(4):
            nc.vector.tensor_copy(g_s[32 * quad : 32 * quad + 4, :].bitcast(I32), stage[:, quad, :].bitcast(I32))
        nc.vector.tensor_copy(wt_wg[:], wt_w[:].indirect(l1[:]))
        nc.vector.tensor_copy(
            wt_wd[:].rearrange("p (t c i) -> p c t i", t=4, i=8),
            wt_wg[:].rearrange("p (c i t) -> p c t i", t=4, i=8),
        )
        for h in range(2):
            nc.vector.tensor_copy(xt_wg[h][:], xt_w[:].indirect(l2[:, 8 * h : 8 * h + 8]))
        nc.vector.tensor_copy(wt_sd[:].rearrange("p (t m) -> p m t", t=4), wt_s[:].indirect(l1[:]))
        for h in range(2):
            nc.vector.tensor_copy(xt_sg[h][:], xt_s[:].indirect(l2[:, 8 * h : 8 * h + 8]))

        gT_ps = ps.tile([P, R], F32, name="gT_ps", tag="b0")
        nc.tensor.matmul_mx(gT_ps[:], lhsT=xc_w[:].bitcast(E5M2), lhsT_scale=xc_s, rhs=wg_w[:].bitcast(E4M3),
                            rhs_scale=wg_s, start=True, stop=True)
        gT = sb.tile([P, 4, P], F32, name="gT")
        nc.scalar.activation(gT[:], gT_ps[:].rearrange("q (m t) -> q t m", t=4), ACT.Copy)
        g_ps = ps.tile([P, 4, Q], F32, name="g_ps", tag="b1")
        for t in range(4):
            nc.tensor.transpose(g_ps[:, t, :], gT[:, t, :], ident[:])
        g_sb = sb.tile([P, 4, Q], F32, name="g_sb")
        nc.scalar.copy(g_sb[:], g_ps[:])

        a_sb = [sb.tile([P, J], F32, name="a_sb%d" % t) for t in range(4)]

        def slot_product(dst, t, h):
            nc.tensor.matmul_mx(dst, lhsT=wt_wd[:, P * t : P * (t + 1)].bitcast(E2M1),
                                lhsT_scale=wt_sd[:, P * t : P * (t + 1)], rhs=xt_wg[h][:].bitcast(E5M2),
                                rhs_scale=xt_sg[h][:], start=True, stop=True)

        for h, engine_copy in enumerate((nc.scalar.copy, nc.vector.tensor_copy)):
            a_ps = ps.tile([P, P], F32, name="a_ps0%d" % h, tag="b%d" % h)
            slot_product(a_ps[:], 0, h)
            engine_copy(a_sb[0][:, P * h : P * (h + 1)], a_ps[:])
        for t in range(1, 4):
            a_ps = ps.tile([P, J], F32, name="a_ps%d" % t, tag="b%d" % ((t + 1) % 2))
            for h in range(2):
                slot_product(a_ps[:, P * h : P * (h + 1)], t, h)
            nc.vector.tensor_copy(a_sb[t][:], a_ps[:])

        g_bf = sb.tile([P, Q, 4], BF16, name="g_bf", tag="dealt", align_bytes=64)
        nc.vector.tensor_copy(g_bf[:].rearrange("p (c i) t -> p c t i", i=4), g_sb[:].rearrange("p t (c i) -> p c t i", i=4))
        p_sb = [sb.tile([P, D], F32, name="p_sb%d" % c) for c in range(2)]

        def output_product(x_bf, name, tags, d0):
            codes = sb.tile([P, P], U32, name=name + "_w", align_bytes=64)
            plane = sb.tile([P, P], U8, name=name + "_s", align_bytes=64)
            nc.vector.quantize_mx(codes[:].bitcast(E4M3), plane[:], x_bf[:].rearrange("p d t -> p (d t)"))
            for c in range(2):
                p_ps = ps.tile([P, P], F32, name="%s_ps%d" % (name, c), tag=tags[c])
                nc.tensor.matmul_mx(p_ps[:], lhsT=wb_w[:, P * c : P * (c + 1)].bitcast(E2M1),
                                    lhsT_scale=wb_s[:, P * c : P * (c + 1)], rhs=codes[:].bitcast(E4M3),
                                    rhs_scale=plane[:], start=True, stop=True)
                nc.vector.tensor_copy(p_sb[c][:, d0 : d0 + P], p_ps[:])

        h_bf = sb.tile([P, O, 4], BF16, name="h_bf", align_bytes=64)
        for u in range(2):
            first = sb.tile([P, 2, O], F32, name="first%d" % u)
            second = sb.tile([P, 2, O], F32, name="second%d" % u)
            for s in range(2):
                t = 2 * u + s
                nc.scalar.activation(first[:, s, :], a_sb[t][:].indirect(l3[:]), ACT.Copy, scale=g_sb[:, t, 0:1])
                nc.scalar.activation(second[:, s, :], a_sb[t][:].indirect(l4[:]), ACT.Copy, scale=g_sb[:, t, 64:65])
            nc.vector.tensor_tensor(h_bf[:, :, 2 * u : 2 * u + 2], first[:].rearrange("p s o -> p o s"),
                                    second[:].rearrange("p s o -> p o s"), ALU.max)
            if u == 0:
                output_product(g_bf, "g", ("b2", "b3"), O)
        output_product(h_bf, "h", ("b4", "b5"), 0)

        for c in range(2):
            gate = sb.tile([P, U], F32, name="gate%d" % c)
            val = sb.tile([P, U], F32, name="val%d" % c)
            nc.scalar.activation(gate[:], p_sb[c][:].indirect(l6[:]), ACT.Sigmoid,
                                 bias=cols["bo"][:, c : c + 1], scale=cols["sp"][:, c : c + 1])
            nc.scalar.activation(val[:], p_sb[c][:].indirect(l5[:]), ACT.Copy, scale=cols["so"][:, c : c + 1])
            nc.vector.tensor_tensor(pages[c][:].indirect(l7[:]), val[:], gate[:], ALU.mult)
            nc.sync.dma_start(out[P * c : P * (c + 1), :], pages[c][:])
